import numpy as np
import ml_dtypes


def mxq(x, axis, fmt="e4m3"):
    dtype, down = {"e4m3": (ml_dtypes.float8_e4m3fn, 7), "e5m2": (ml_dtypes.float8_e5m2, 14)}[fmt]
    v = np.moveaxis(np.asarray(x, np.float32).astype(ml_dtypes.bfloat16).astype(np.float64), axis, -1)
    blocks = v.reshape(v.shape[:-1] + (-1, 32))
    amax = np.abs(blocks).max(-1, keepdims=True)
    byte = np.maximum(np.where(amax > 0, np.frexp(amax)[1] - 1 + 127, 0) - down, 1)
    scale = np.exp2(byte - 127.0)
    codes = (blocks / scale).astype(np.float32).astype(dtype).astype(np.float64)
    return np.moveaxis((codes * scale).reshape(v.shape), -1, axis)


WIDE = False


def mx_kscale(k):
    if not WIDE:
        return np.ones(k)
    levels = np.array([10, -10, 5, -5, 0])
    if k % 512:
        return np.exp2(np.random.permutation(np.resize(levels, k // 32))).repeat(32)
    a = np.empty((k // 512, 16))
    for p in range(k // 512):
        a[p, :8] = np.random.permutation(np.resize(levels, 8))
        for g in range(8):
            far = levels[np.abs(levels - a[p, g]) >= 10]
            a[p, g + 8] = far[np.random.randint(len(far))]
    return np.exp2(a.ravel()).repeat(32)


def f64(x):
    return np.asarray(x).astype(np.float64)


def striped(idx):
    return np.tile(idx.reshape(-1, 16).T, (8, 1)).astype(np.uint16)


def unstriped(offs):
    return offs[:16].T.reshape(-1).astype(np.int64)


def striped8(idx):
    return np.concatenate([x.reshape(-1, 16).T for x in idx]).astype(np.uint16)


def runs(offs, k):
    lists = np.stack([offs[16 * r : 16 * r + 16].T.reshape(-1) for r in range(8)]).astype(np.int64)
    return lists[np.arange(k) % 512 // 64]


def pack_weight(w):
    k, n = w.shape
    w = f64(np.asarray(w, np.float32).astype(ml_dtypes.bfloat16)).reshape(k // 32, 32, n)
    amax = np.abs(w).max(1)
    byte = np.clip(np.where(amax > 0, np.frexp(amax)[1] - 1 + 127 - 7, 1), 1, 254)
    scaled = (w * np.exp2(127.0 - byte)[:, None, :]).reshape(k, n).astype(np.float32)
    words = np.ascontiguousarray(scaled.reshape(k // 512, 128, 4, n).transpose(0, 1, 3, 2)).astype(ml_dtypes.float8_e4m3fn).view(np.uint8)
    return words, np.ascontiguousarray(byte.astype(np.uint8).reshape(k // 512, 16, n))


def unpack_weight(words, scales):
    g, p, n, _ = words.shape
    vals = np.ascontiguousarray(words).view(ml_dtypes.float8_e4m3fn).astype(np.float64) * np.repeat(np.exp2(scales.astype(np.float64) - 127.0), 8, axis=1)[..., None]
    return vals.transpose(0, 1, 3, 2).reshape(g * 512, n)

def planes(y):
    n, m = y.shape
    v = y.astype(np.float32).astype(ml_dtypes.bfloat16).astype(np.float64).reshape(n // 32, 32, m)
    top = np.abs(v).max(1)
    byte = np.clip(np.where(top > 0, np.frexp(top)[1] - 1 + 127 - 7, 1), 1, 254)
    codes = (v * np.exp2(127.0 - byte)[:, None, :]).reshape(n, m).astype(np.float32).astype(ml_dtypes.float8_e4m3fn).view(np.uint8)
    words = codes.reshape(n // 512, 128, 4, m).transpose(0, 1, 3, 2)
    return np.ascontiguousarray(words), np.ascontiguousarray(byte.astype(np.uint8).reshape(n // 512, 16, m))


K, T, S, N, H, G, W = 512, 2048, 512, 512, 512, 2048, 256


def setup_inputs():
    n = np.random.standard_normal
    s = mx_kscale(K)[:, None]
    u = mx_kscale(S)
    packed_xT = pack_weight(n((K, T)) * s)
    packed_w1 = pack_weight(n((K, H)) / np.sqrt(K) / s)
    packed_dT = pack_weight(n((K, G)) / s)
    packed_w2 = pack_weight(n((H, N)) / np.sqrt(H) / u[:, None])
    perm = np.stack([np.random.permutation(S) for _ in range(8)])
    return {
        "x_words": packed_xT[0],
        "x_scales": packed_xT[1],
        "w1_words": packed_w1[0],
        "w1_scales": packed_w1[1],
        "d_words": packed_dT[0],
        "d_scales": packed_dT[1],
        "gn": (np.random.uniform(0.5, 1.5, (H, 1)) * u[:, None]).astype(np.float32),
        "w2_words": packed_w2[0],
        "w2_scales": packed_w2[1],
        "offs": striped(np.random.permutation(T)[:S]),
        "k1": striped8(np.random.randint(0, G, (8, H))),
        "two": striped(np.random.permutation(T)[:S]),
        "n1": striped(np.random.permutation(S)),
        "n2": striped(np.random.permutation(S)),
        "n3": striped8(perm[:, :W]),
        "n4": striped8(perm[:, W:]),
    }


def reference(x_words, x_scales, w1_words, w1_scales, d_words, d_scales, gn, w2_words, w2_scales, offs, k1, two, n1, n2, n3, n4):
    xq = unpack_weight(x_words, x_scales)[:, unstriped(offs)]
    y = unpack_weight(w1_words, w1_scales).T @ xq
    d_k1 = unpack_weight(d_words, d_scales)[np.arange(K)[:, None], runs(k1, K)]
    x_two = unpack_weight(x_words, x_scales)[:, unstriped(two)]
    d = 0.0625 * (d_k1.T @ x_two)
    z = f64(gn) * (y[:, unstriped(n1)] - (np.tanh(d) * d[:, unstriped(n2)]))
    h = unpack_weight(w2_words, w2_scales).T @ mxq(z, 0, "e4m3")
    pb = h[np.arange(N)[:, None], runs(n4, N)]
    pa = h[np.arange(N)[:, None], runs(n3, N)]
    rb = pb - (0.5 * pa)
    ra = np.sqrt((pa) ** 2 + (pb) ** 2 + 0.25)
    ds = np.zeros((N, S))
    ds[np.arange(N)[:, None], runs(n3, N)] = ra
    out = ds.copy()
    out[np.arange(N)[:, None], runs(n4, N)] = rb
    return (out,) + planes(out)

@@ -1,0 +1,229 @@
+from contextlib import ExitStack
+
+import concourse.mybir as mybir
+
+F32 = mybir.dt.float32
+BF16 = mybir.dt.bfloat16
+I32 = mybir.dt.int32
+U32 = mybir.dt.uint32
+U16 = mybir.dt.uint16
+U8 = mybir.dt.uint8
+FP8X4 = mybir.dt.float8_e4m3fn_x4
+ALU = mybir.AluOpType
+ACT = mybir.ActivationFunctionType
+
+P = 128
+PACK = 4
+TABLE = 2048
+S = 512
+PAIRS = 256
+SPARE = 8
+HALVES = 2
+FLOPS = 3 * 2 * 512 * 512 * 512
+
+
+def tile_picked_twkeysoftbpolar_none_po_kernel(
+    tc, x_words, x_scales, w1_words, w1_scales, d_words, d_scales, gn, w2_words, w2_scales,
+    offs, k1, two, n1, n2, n3, n4, out_0, out_1, out_2,
+):
+    nc = tc.nc
+    half = S // HALVES
+
+    def words_of(dram):
+        return dram[0].rearrange("p c t -> p (c t)").bitcast(I32)
+
+    with ExitStack() as ctx:
+        keep = ctx.enter_context(tc.tile_pool(name="keep", bufs=1))
+        psum = ctx.enter_context(tc.psum_pool(name="psum", bufs=1))
+
+        def new(shape, dtype, name):
+            return keep.tile(shape, dtype, name=name, align_bytes=64)
+
+        def load_list(dram, name):
+            tile = new(list(dram.shape), U16, name)
+            nc.sync.dma_start(tile[:], dram)
+            return tile
+
+        def load_scale_rows(queue, tile, dram):
+            rows = dram[0].bitcast(I32)
+            for j in range(PACK):
+                queue.dma_start(tile[:].bitcast(I32)[j:P:32, :], rows[j:16:PACK, :])
+
+        def deal(out, in_):
+            nc.vector.tensor_copy(out.rearrange("p (t m) -> p m t", t=PACK), in_.rearrange("p (m t) -> p m t", t=PACK))
+
+        d_byte_table = new([P, TABLE], U8, "d_byte_table")
+        x_byte_table = new([P, TABLE], U8, "x_byte_table")
+        w_bytes_raw = new([P, S], U8, "w_bytes_raw")
+        nc.gpsimd.memset(x_byte_table[:].bitcast(I32), 0)
+        nc.gpsimd.memset(w_bytes_raw[:].bitcast(I32), 0)
+
+        d_word_table = new([P, TABLE], U32, "d_word_table")
+        x_word_table = new([P, TABLE], U32, "x_word_table")
+        w_words_raw = new([P, S], U32, "w_words_raw")
+        gain = new([P, PACK], F32, "gain")
+
+        k1_list = load_list(k1, "k1_list")
+        d_rows = d_scales[0].bitcast(I32)
+        for j in range(2):
+            repeated = d_rows[j:16:2, :].unsqueeze(1).broadcast_to([8, 8, TABLE // 4])
+            nc.sync.dma_start(d_byte_table[:].bitcast(I32)[j:P:2, :], repeated)
+        two_list = load_list(two, "two_list")
+        offs_list = load_list(offs, "offs_list")
+        n2_list = load_list(n2, "n2_list")
+        n1_list = load_list(n1, "n1_list")
+        nc.sync.dma_start(d_word_table[:].bitcast(I32), words_of(d_words))
+        load_scale_rows(nc.sync, x_byte_table, x_scales)
+        nc.sync.dma_start(x_word_table[:].bitcast(I32), words_of(x_words))
+        n3_list = load_list(n3, "n3_list")
+        n4_list = load_list(n4, "n4_list")
+        nc.sync.dma_start(w_words_raw[:].bitcast(I32), words_of(w1_words))
+        nc.sync.dma_start(gain[:], gn.rearrange("(p t) o -> p (t o)", t=PACK))
+        load_scale_rows(nc.sync, w_bytes_raw, w1_scales)
+
+        gain16 = new([P, PACK], F32, "gain16")
+        nc.scalar.activation(gain16[:], gain[:], ACT.Copy, scale=0.0625)
+
+        def gather(table, offsets, dtype, name):
+            picked = new([P, S], dtype, name)
+            nc.vector.tensor_copy(picked[:], table[:].indirect(offsets[:]))
+            return picked
+
+        d_bytes_picked = gather(d_byte_table, k1_list, U8, "d_bytes_picked")
+        d_bytes = new([P, S], U8, "d_bytes")
+        deal(d_bytes[:], d_bytes_picked[:])
+        for j in range(2):
+            nc.scalar.dma_start(d_bytes[:].bitcast(I32)[2 + j : P : 32, :], d_bytes[:].bitcast(I32)[16 + j : P : 32, :])
+        d_words_picked = gather(d_word_table, k1_list, U32, "d_words_picked")
+        d_codes = new([P, S], U32, "d_codes")
+        deal(d_codes[:], d_words_picked[:])
+        x2_bytes = gather(x_byte_table, two_list, U8, "x2_bytes")
+        x2_codes = gather(x_word_table, two_list, U32, "x2_codes")
+
+        def product(bank, codes, scale_bytes, t, moving_codes, moving_bytes):
+            cols = slice(t * P, (t + 1) * P)
+            nc.tensor.matmul_mx(
+                out=bank, lhsT=codes[:, cols].bitcast(FP8X4), lhsT_scale=scale_bytes[:, cols],
+                rhs=moving_codes.bitcast(FP8X4), rhs_scale=moving_bytes, start=True, stop=True,
+            )
+
+        d_window, tanh_neg = [], []
+        for t in range(PACK):
+            bank = psum.tile([P, S], F32, name=f"d_bank{t}", tag=f"bank{t}")
+            product(bank[:], d_codes, d_bytes, t, x2_codes[:], x2_bytes[:])
+            d_window.append(new([P, S + SPARE], F32, f"d_window{t}"))
+            nc.gpsimd.memset(d_window[t][:, S:], 0.0)
+            nc.scalar.activation(d_window[t][:, :S], bank[:], ACT.Copy, scale=gain16[:, t : t + 1])
+            tanh_neg.append(new([P, S], F32, f"tanh_neg{t}"))
+            nc.scalar.activation(tanh_neg[t][:], bank[:], ACT.Tanh, scale=-0.0625)
+
+        w1_codes = new([P, S], U32, "w1_codes")
+        w1_bytes = new([P, S], U8, "w1_bytes")
+        x1_bytes = gather(x_byte_table, offs_list, U8, "x1_bytes")
+        deal(w1_codes[:], w_words_raw[:])
+        deal(w1_bytes[:], w_bytes_raw[:])
+        nc.sync.dma_start(w_words_raw[:].bitcast(I32), words_of(w2_words))
+        load_scale_rows(nc.sync, w_bytes_raw, w2_scales)
+        x1_codes = gather(x_word_table, offs_list, U32, "x1_codes")
+
+        y_bank = []
+        for t in range(PACK):
+            y_bank.append(psum.tile([P, S], F32, name=f"y_bank{t}", tag=f"bank{PACK + t}"))
+            product(y_bank[t][:], w1_codes, w1_bytes, t, x1_codes[:], x1_bytes[:])
+
+        cross = new([P, PACK, S], F32, "cross")
+        y_window = []
+        for t in range(PACK):
+            nc.vector.tensor_tensor(cross[:, t, :], d_window[t][:].indirect(n2_list[:]), tanh_neg[t][:], ALU.mult)
+            y_window.append(new([P, S], F32, f"y_window{t}"))
+            if t < PACK - 1:
+                nc.vector.tensor_scalar(y_window[t][:], y_bank[t][:], gain[:, t : t + 1], None, ALU.mult)
+            else:
+                nc.scalar.activation(y_window[t][:], y_bank[t][:], ACT.Copy, scale=gain[:, t : t + 1])
+
+        w2_codes = new([P, S], U32, "w2_codes")
+        w2_bytes = new([P, S], U8, "w2_bytes")
+        z_codes = new([P, S], U32, "z_codes")
+        z_bytes = new([P, S], U8, "z_bytes")
+        deal(w2_codes[:], w_words_raw[:])
+        deal(w2_bytes[:], w_bytes_raw[:])
+        y_picked = []
+        for u in range(HALVES):
+            y_picked.append(new([P, PACK, half], F32, f"y_picked{u}"))
+            for t in range(PACK):
+                offsets = n1_list[:, u * half // 16 : (u + 1) * half // 16]
+                nc.scalar.activation(y_picked[u][:, t, :], y_window[t][:].indirect(offsets), ACT.Copy)
+        h_window = [new([P, S], F32, f"h_window{t}") for t in range(PACK)]
+        h_bank = {}
+        for u in range(HALVES):
+            cols = slice(u * half, (u + 1) * half)
+            z_rounded = new([P, half, PACK], BF16, f"z_rounded{u}")
+            nc.vector.tensor_tensor(
+                z_rounded[:].rearrange("p (c i) t -> p c t i", i=4),
+                y_picked[u][:].rearrange("p t (c i) -> p c t i", i=4),
+                cross[:, :, cols].rearrange("p t (c i) -> p c t i", i=4),
+                ALU.add,
+            )
+            nc.vector.quantize_mx(
+                out=z_codes[:, cols].bitcast(FP8X4), scales=z_bytes[:, cols],
+                in_=z_rounded[:].rearrange("p c t -> p (c t)"),
+            )
+            for t in range(PACK):
+                h_bank[u, t] = psum.tile([P, half], F32, name=f"h_bank{u}_{t}", tag=f"bank{u * PACK + t}")
+                product(h_bank[u, t][:], w2_codes, w2_bytes, t, z_codes[:, cols], z_bytes[:, cols])
+                if u == 0:
+                    nc.scalar.copy(h_window[t][:, cols], h_bank[u, t][:])
+
+        out_rows = out_0.rearrange("(p t) c -> p t c", t=PACK)
+        out_planes = new([P, PACK, S], BF16, "out_planes")
+        placed = [new([P, S], F32, f"placed{t}") for t in range(PACK)]
+        total = [new([P, PAIRS], F32, f"total{t}") for t in range(PACK)]
+
+        def pair_up(t):
+            nc.scalar.copy(h_window[t][:, half:], h_bank[1, t][:])
+            pair = new([P, 2, PAIRS], F32, f"pair{t}")
+            nc.scalar.activation(pair[:, 0, :], h_window[t][:].indirect(n3_list[:]), ACT.Copy, scale=-0.5)
+            if t == 0:
+                nc.vector.tensor_copy(pair[:, 1, :], h_window[t][:].indirect(n4_list[:]))
+            else:
+                nc.scalar.activation(pair[:, 1, :], h_window[t][:].indirect(n4_list[:]), ACT.Copy)
+            nc.vector.tensor_tensor(placed[t][:].indirect(n4_list[:]), pair[:, 1, :], pair[:, 0, :], ALU.add)
+            squares = new([P, 2, PAIRS], F32, f"squares{t}")
+            nc.scalar.activation(squares[:], pair[:], ACT.Square)
+            nc.vector.scalar_tensor_tensor(total[t][:], squares[:, 0, :], 4.0, squares[:, 1, :], ALU.mult, ALU.add)
+
+        def place_roots(t):
+            root = new([P, PAIRS], F32, f"root{t}")
+            nc.scalar.activation(root[:], total[t][:], ACT.Sqrt, bias=0.25)
+            nc.vector.tensor_copy(placed[t][:].indirect(n3_list[:]), root[:])
+            nc.sync.dma_start(out_rows[:, t, :], placed[t][:])
+
+        pair_up(0)
+        for t in range(1, PACK):
+            pair_up(t)
+            place_roots(t - 1)
+        place_roots(PACK - 1)
+        for t in range(PACK - 1):
+            nc.scalar.copy(out_planes[:, t, :], placed[t][:])
+        nc.vector.tensor_copy(out_planes[:, PACK - 1, :], placed[PACK - 1][:])
+
+        out_rounded = new([P, S, PACK], BF16, "out_rounded")
+        out_codes = new([P, S], U32, "out_codes")
+        out_bytes = new([P, S], U8, "out_bytes")
+        walk_out = out_rounded[:].rearrange("p (c i) t -> p c t i", i=4)
+        walk_in = out_planes[:].rearrange("p t (c i) -> p c t i", i=4)
+        groups = S // 4
+        nc.vector.tensor_copy(walk_out[:, : groups // 2], walk_in[:, : groups // 2])
+        nc.scalar.copy(walk_out[:, 3 * groups // 4 :], walk_in[:, 3 * groups // 4 :])
+        nc.vector.tensor_copy(walk_out[:, groups // 2 : 3 * groups // 4], walk_in[:, groups // 2 : 3 * groups // 4])
+        for u in range(HALVES):
+            cols = slice(u * half, (u + 1) * half)
+            nc.vector.quantize_mx(
+                out=out_codes[:, cols].bitcast(FP8X4), scales=out_bytes[:, cols],
+                in_=out_rounded[:, cols, :].rearrange("p c t -> p (c t)"),
+            )
+            nc.sync.dma_start(words_of(out_1)[:, cols], out_codes[:].bitcast(I32)[:, cols])
+        scale_rows = out_2[0].bitcast(I32)
+        for q in range(4):
+            queue = nc.scalar if q % 2 else nc.sync
+            queue.dma_start(scale_rows[4 * q : 4 * q + 4, :], out_bytes[:].bitcast(I32)[32 * q : 32 * q + 4, :])

@@ -49,18 +49,21 @@ def tile_picked_twkeysoftbpolar_none_po_kernel(
             for j in range(PACK):
                 queue.dma_start(tile[:].bitcast(I32)[j:P:32, :], rows[j:16:PACK, :])
 
-        def deal(out, in_):
-            nc.vector.tensor_copy(out.rearrange("p (t m) -> p m t", t=PACK), in_.rearrange("p (m t) -> p m t", t=PACK))
+        def deal(out, in_, engine=nc.vector):
+            engine.tensor_copy(out.rearrange("p (t m) -> p m t", t=PACK), in_.rearrange("p (m t) -> p m t", t=PACK))
 
         d_byte_table = new([P, TABLE], U8, "d_byte_table")
         x_byte_table = new([P, TABLE], U8, "x_byte_table")
-        w_bytes_raw = new([P, S], U8, "w_bytes_raw")
+        w1_bytes_raw = new([P, S], U8, "w1_bytes_raw")
+        w2_bytes_raw = new([P, S], U8, "w2_bytes_raw")
         nc.gpsimd.memset(x_byte_table[:].bitcast(I32), 0)
-        nc.gpsimd.memset(w_bytes_raw[:].bitcast(I32), 0)
+        nc.gpsimd.memset(w1_bytes_raw[:].bitcast(I32), 0)
+        nc.gpsimd.memset(w2_bytes_raw[:].bitcast(I32), 0)
 
         d_word_table = new([P, TABLE], U32, "d_word_table")
         x_word_table = new([P, TABLE], U32, "x_word_table")
-        w_words_raw = new([P, S], U32, "w_words_raw")
+        w1_words_raw = new([P, S], U32, "w1_words_raw")
+        w2_words_raw = new([P, S], U32, "w2_words_raw")
         gain = new([P, PACK], F32, "gain")
 
         k1_list = load_list(k1, "k1_list")
@@ -69,17 +72,19 @@ def tile_picked_twkeysoftbpolar_none_po_kernel(
             repeated = d_rows[j:16:2, :].unsqueeze(1).broadcast_to([8, 8, TABLE // 4])
             nc.sync.dma_start(d_byte_table[:].bitcast(I32)[j:P:2, :], repeated)
         two_list = load_list(two, "two_list")
-        offs_list = load_list(offs, "offs_list")
         n2_list = load_list(n2, "n2_list")
         n1_list = load_list(n1, "n1_list")
+        n3_list = load_list(n3, "n3_list")
         nc.sync.dma_start(d_word_table[:].bitcast(I32), words_of(d_words))
         load_scale_rows(nc.sync, x_byte_table, x_scales)
         nc.sync.dma_start(x_word_table[:].bitcast(I32), words_of(x_words))
-        n3_list = load_list(n3, "n3_list")
+        offs_list = load_list(offs, "offs_list")
+        nc.sync.dma_start(w1_words_raw[:].bitcast(I32), words_of(w1_words))
+        load_scale_rows(nc.sync, w1_bytes_raw, w1_scales)
         n4_list = load_list(n4, "n4_list")
-        nc.sync.dma_start(w_words_raw[:].bitcast(I32), words_of(w1_words))
-        nc.sync.dma_start(gain[:], gn.rearrange("(p t) o -> p (t o)", t=PACK))
-        load_scale_rows(nc.sync, w_bytes_raw, w1_scales)
+        nc.gpsimd.dma_start(gain[:], gn.rearrange("(p t) o -> p (t o)", t=PACK))
+        load_scale_rows(nc.gpsimd, w2_bytes_raw, w2_scales)
+        nc.gpsimd.dma_start(w2_words_raw[:].bitcast(I32), words_of(w2_words))
 
         gain16 = new([P, PACK], F32, "gain16")
         nc.scalar.activation(gain16[:], gain[:], ACT.Copy, scale=0.0625)
@@ -119,12 +124,10 @@ def tile_picked_twkeysoftbpolar_none_po_kernel(
 
         w1_codes = new([P, S], U32, "w1_codes")
         w1_bytes = new([P, S], U8, "w1_bytes")
-        x1_bytes = gather(x_byte_table, offs_list, U8, "x1_bytes")
-        deal(w1_codes[:], w_words_raw[:])
-        deal(w1_bytes[:], w_bytes_raw[:])
-        nc.sync.dma_start(w_words_raw[:].bitcast(I32), words_of(w2_words))
-        load_scale_rows(nc.sync, w_bytes_raw, w2_scales)
         x1_codes = gather(x_word_table, offs_list, U32, "x1_codes")
+        x1_bytes = gather(x_byte_table, offs_list, U8, "x1_bytes")
+        deal(w1_codes[:], w1_words_raw[:])
+        deal(w1_bytes[:], w1_bytes_raw[:])
 
         y_bank = []
         for t in range(PACK):
@@ -132,21 +135,21 @@ def tile_picked_twkeysoftbpolar_none_po_kernel(
             product(y_bank[t][:], w1_codes, w1_bytes, t, x1_codes[:], x1_bytes[:])
 
         cross = new([P, PACK, S], F32, "cross")
-        y_window = []
+        y_window = [new([P, S], F32, f"y_window{t}") for t in range(PACK)]
         for t in range(PACK):
+            if t == 2:
+                for late in (2, 3):
+                    nc.vector.tensor_scalar(y_window[late][:], y_bank[late][:], gain[:, late : late + 1], None, ALU.mult)
             nc.vector.tensor_tensor(cross[:, t, :], d_window[t][:].indirect(n2_list[:]), tanh_neg[t][:], ALU.mult)
-            y_window.append(new([P, S], F32, f"y_window{t}"))
-            if t < PACK - 1:
-                nc.vector.tensor_scalar(y_window[t][:], y_bank[t][:], gain[:, t : t + 1], None, ALU.mult)
-            else:
-                nc.scalar.activation(y_window[t][:], y_bank[t][:], ACT.Copy, scale=gain[:, t : t + 1])
+        for t in range(2):
+            nc.scalar.activation(y_window[t][:], y_bank[t][:], ACT.Copy, scale=gain[:, t : t + 1])
 
         w2_codes = new([P, S], U32, "w2_codes")
-        w2_bytes = new([P, S], U8, "w2_bytes")
         z_codes = new([P, S], U32, "z_codes")
         z_bytes = new([P, S], U8, "z_bytes")
-        deal(w2_codes[:], w_words_raw[:])
-        deal(w2_bytes[:], w_bytes_raw[:])
+        w2_bytes = new([P, S], U8, "w2_bytes")
+        deal(w2_bytes[:], w2_bytes_raw[:], nc.gpsimd)
+        deal(w2_codes[:], w2_words_raw[:], nc.gpsimd)
         y_picked = []
         for u in range(HALVES):
             y_picked.append(new([P, PACK, half], F32, f"y_picked{u}"))
@@ -179,17 +182,20 @@ def tile_picked_twkeysoftbpolar_none_po_kernel(
         placed = [new([P, S], F32, f"placed{t}") for t in range(PACK)]
         total = [new([P, PAIRS], F32, f"total{t}") for t in range(PACK)]
 
-        def pair_up(t):
+        pair = [new([P, 2, PAIRS], F32, f"pair{t}") for t in range(PACK)]
+
+        def place_differences(t):
             nc.scalar.copy(h_window[t][:, half:], h_bank[1, t][:])
-            pair = new([P, 2, PAIRS], F32, f"pair{t}")
-            nc.scalar.activation(pair[:, 0, :], h_window[t][:].indirect(n3_list[:]), ACT.Copy, scale=-0.5)
+            nc.scalar.activation(pair[t][:, 0, :], h_window[t][:].indirect(n3_list[:]), ACT.Copy, scale=-0.5)
             if t == 0:
-                nc.vector.tensor_copy(pair[:, 1, :], h_window[t][:].indirect(n4_list[:]))
+                nc.vector.tensor_copy(pair[t][:, 1, :], h_window[t][:].indirect(n4_list[:]))
             else:
-                nc.scalar.activation(pair[:, 1, :], h_window[t][:].indirect(n4_list[:]), ACT.Copy)
-            nc.vector.tensor_tensor(placed[t][:].indirect(n4_list[:]), pair[:, 1, :], pair[:, 0, :], ALU.add)
+                nc.scalar.activation(pair[t][:, 1, :], h_window[t][:].indirect(n4_list[:]), ACT.Copy)
+            nc.vector.tensor_tensor(placed[t][:].indirect(n4_list[:]), pair[t][:, 1, :], pair[t][:, 0, :], ALU.add)
+
+        def sum_squares(t):
             squares = new([P, 2, PAIRS], F32, f"squares{t}")
-            nc.scalar.activation(squares[:], pair[:], ACT.Square)
+            nc.scalar.activation(squares[:], pair[t][:], ACT.Square)
             nc.vector.scalar_tensor_tensor(total[t][:], squares[:, 0, :], 4.0, squares[:, 1, :], ALU.mult, ALU.add)
 
         def place_roots(t):
@@ -198,11 +204,18 @@ def tile_picked_twkeysoftbpolar_none_po_kernel(
             nc.vector.tensor_copy(placed[t][:].indirect(n3_list[:]), root[:])
             nc.sync.dma_start(out_rows[:, t, :], placed[t][:])
 
-        pair_up(0)
-        for t in range(1, PACK):
-            pair_up(t)
-            place_roots(t - 1)
-        place_roots(PACK - 1)
+        place_differences(0)
+        place_differences(1)
+        sum_squares(0)
+        sum_squares(1)
+        place_differences(2)
+        place_roots(0)
+        place_roots(1)
+        sum_squares(2)
+        place_differences(3)
+        sum_squares(3)
+        place_roots(2)
+        place_roots(3)
         for t in range(PACK - 1):
             nc.scalar.copy(out_planes[:, t, :], placed[t][:])
         nc.vector.tensor_copy(out_planes[:, PACK - 1, :], placed[PACK - 1][:])

@@ -36,8 +36,8 @@ def tile_picked_twkeysoftbpolar_none_po_kernel(
         keep = ctx.enter_context(tc.tile_pool(name="keep", bufs=1))
         psum = ctx.enter_context(tc.psum_pool(name="psum", bufs=1))
 
-        def new(shape, dtype, name):
-            return keep.tile(shape, dtype, name=name, align_bytes=64)
+        def new(shape, dtype, name, tag=None):
+            return keep.tile(shape, dtype, name=name, tag=tag or name, align_bytes=64)
 
         def load_list(dram, name):
             tile = new(list(dram.shape), U16, name)
@@ -160,7 +160,7 @@ def tile_picked_twkeysoftbpolar_none_po_kernel(
         h_bank = {}
         for u in range(HALVES):
             cols = slice(u * half, (u + 1) * half)
-            z_rounded = new([P, half, PACK], BF16, f"z_rounded{u}")
+            z_rounded = new([P, half, PACK], BF16, f"z_rounded{u}", tag="z_rounded")
             nc.vector.tensor_tensor(
                 z_rounded[:].rearrange("p (c i) t -> p c t i", i=4),
                 y_picked[u][:].rearrange("p t (c i) -> p c t i", i=4),
@@ -207,18 +207,20 @@ def tile_picked_twkeysoftbpolar_none_po_kernel(
         place_differences(0)
         place_differences(1)
         sum_squares(0)
-        sum_squares(1)
         place_differences(2)
         place_roots(0)
-        place_roots(1)
-        sum_squares(2)
+        sum_squares(1)
         place_differences(3)
+        sum_squares(2)
+        place_roots(1)
         sum_squares(3)
         place_roots(2)
         place_roots(3)
         for t in range(PACK - 1):
             nc.scalar.copy(out_planes[:, t, :], placed[t][:])
-        nc.vector.tensor_copy(out_planes[:, PACK - 1, :], placed[PACK - 1][:])
+        split = 3 * S // 4
+        nc.vector.tensor_copy(out_planes[:, PACK - 1, :split], placed[PACK - 1][:, :split])
+        nc.scalar.copy(out_planes[:, PACK - 1, split:], placed[PACK - 1][:, split:])
 
         out_rounded = new([P, S, PACK], BF16, "out_rounded")
         out_codes = new([P, S], U32, "out_codes")

@@ -195,8 +195,13 @@ def tile_picked_twkeysoftbpolar_none_po_kernel(
 
         def sum_squares(t):
             squares = new([P, 2, PAIRS], F32, f"squares{t}")
-            nc.scalar.activation(squares[:], pair[t][:], ACT.Square)
-            nc.vector.scalar_tensor_tensor(total[t][:], squares[:, 0, :], 4.0, squares[:, 1, :], ALU.mult, ALU.add)
+            if t == 0:
+                nc.scalar.activation(squares[:], pair[t][:], ACT.Square)
+                nc.vector.scalar_tensor_tensor(total[t][:], squares[:, 0, :], 4.0, squares[:, 1, :], ALU.mult, ALU.add)
+            else:
+                nc.scalar.activation(squares[:, 0, :], pair[t][:, 0, :], ACT.Square, scale=2.0)
+                nc.scalar.activation(squares[:, 1, :], pair[t][:, 1, :], ACT.Square)
+                nc.gpsimd.tensor_tensor(total[t][:], squares[:, 0, :], squares[:, 1, :], ALU.add)
 
         def place_roots(t):
             root = new([P, PAIRS], F32, f"root{t}")
@@ -218,7 +223,7 @@ def tile_picked_twkeysoftbpolar_none_po_kernel(
         place_roots(3)
         for t in range(PACK - 1):
             nc.scalar.copy(out_planes[:, t, :], placed[t][:])
-        split = 3 * S // 4
+        split = 336
         nc.vector.tensor_copy(out_planes[:, PACK - 1, :split], placed[PACK - 1][:, :split])
         nc.scalar.copy(out_planes[:, PACK - 1, split:], placed[PACK - 1][:, split:])
 
@@ -227,12 +232,9 @@ def tile_picked_twkeysoftbpolar_none_po_kernel(
         out_bytes = new([P, S], U8, "out_bytes")
         walk_out = out_rounded[:].rearrange("p (c i) t -> p c t i", i=4)
         walk_in = out_planes[:].rearrange("p t (c i) -> p c t i", i=4)
-        groups = S // 4
-        nc.vector.tensor_copy(walk_out[:, : groups // 2], walk_in[:, : groups // 2])
-        nc.scalar.copy(walk_out[:, 3 * groups // 4 :], walk_in[:, 3 * groups // 4 :])
-        nc.vector.tensor_copy(walk_out[:, groups // 2 : 3 * groups // 4], walk_in[:, groups // 2 : 3 * groups // 4])
-        for u in range(HALVES):
-            cols = slice(u * half, (u + 1) * half)
+        nc.vector.tensor_copy(walk_out[:, : split // 4], walk_in[:, : split // 4])
+        nc.scalar.copy(walk_out[:, split // 4 :], walk_in[:, split // 4 :])
+        for cols in (slice(0, half), slice(half, S)):
             nc.vector.quantize_mx(
                 out=out_codes[:, cols].bitcast(FP8X4), scales=out_bytes[:, cols],
                 in_=out_rounded[:, cols, :].rearrange("p c t -> p (c t)"),

from contextlib import ExitStack

import concourse.mybir as mybir

F32 = mybir.dt.float32
BF16 = mybir.dt.bfloat16
I32 = mybir.dt.int32
U32 = mybir.dt.uint32
U16 = mybir.dt.uint16
U8 = mybir.dt.uint8
FP8X4 = mybir.dt.float8_e4m3fn_x4
ALU = mybir.AluOpType
ACT = mybir.ActivationFunctionType

P = 128
PACK = 4
TABLE = 2048
S = 512
PAIRS = 256
SPARE = 8
HALVES = 2
FLOPS = 3 * 2 * 512 * 512 * 512


def tile_picked_twkeysoftbpolar_none_po_kernel(
    tc, x_words, x_scales, w1_words, w1_scales, d_words, d_scales, gn, w2_words, w2_scales,
    offs, k1, two, n1, n2, n3, n4, out_0, out_1, out_2,
):
    nc = tc.nc
    half = S // HALVES

    def words_of(dram):
        return dram[0].rearrange("p c t -> p (c t)").bitcast(I32)

    with ExitStack() as ctx:
        keep = ctx.enter_context(tc.tile_pool(name="keep", bufs=1))
        psum = ctx.enter_context(tc.psum_pool(name="psum", bufs=1))

        def new(shape, dtype, name, tag=None):
            return keep.tile(shape, dtype, name=name, tag=tag or name, align_bytes=64)

        def load_list(dram, name):
            tile = new(list(dram.shape), U16, name)
            nc.sync.dma_start(tile[:], dram)
            return tile

        def load_scale_rows(queue, tile, dram):
            rows = dram[0].bitcast(I32)
            for j in range(PACK):
                queue.dma_start(tile[:].bitcast(I32)[j:P:32, :], rows[j:16:PACK, :])

        def deal(out, in_, engine=nc.vector):
            engine.tensor_copy(out.rearrange("p (t m) -> p m t", t=PACK), in_.rearrange("p (m t) -> p m t", t=PACK))

        d_byte_table = new([P, TABLE], U8, "d_byte_table")
        x_byte_table = new([P, TABLE], U8, "x_byte_table")
        w1_bytes_raw = new([P, S], U8, "w1_bytes_raw")
        w2_bytes_raw = new([P, S], U8, "w2_bytes_raw")
        nc.gpsimd.memset(x_byte_table[:].bitcast(I32), 0)
        nc.gpsimd.memset(w1_bytes_raw[:].bitcast(I32), 0)
        nc.gpsimd.memset(w2_bytes_raw[:].bitcast(I32), 0)

        d_word_table = new([P, TABLE], U32, "d_word_table")
        x_word_table = new([P, TABLE], U32, "x_word_table")
        w1_words_raw = new([P, S], U32, "w1_words_raw")
        w2_words_raw = new([P, S], U32, "w2_words_raw")
        gain = new([P, PACK], F32, "gain")

        k1_list = load_list(k1, "k1_list")
        d_rows = d_scales[0].bitcast(I32)
        for j in range(2):
            repeated = d_rows[j:16:2, :].unsqueeze(1).broadcast_to([8, 8, TABLE // 4])
            nc.sync.dma_start(d_byte_table[:].bitcast(I32)[j:P:2, :], repeated)
        two_list = load_list(two, "two_list")
        n2_list = load_list(n2, "n2_list")
        n1_list = load_list(n1, "n1_list")
        n3_list = load_list(n3, "n3_list")
        nc.sync.dma_start(d_word_table[:].bitcast(I32), words_of(d_words))
        load_scale_rows(nc.sync, x_byte_table, x_scales)
        nc.sync.dma_start(x_word_table[:].bitcast(I32), words_of(x_words))
        offs_list = load_list(offs, "offs_list")
        nc.sync.dma_start(w1_words_raw[:].bitcast(I32), words_of(w1_words))
        load_scale_rows(nc.sync, w1_bytes_raw, w1_scales)
        n4_list = load_list(n4, "n4_list")
        nc.gpsimd.dma_start(gain[:], gn.rearrange("(p t) o -> p (t o)", t=PACK))
        load_scale_rows(nc.gpsimd, w2_bytes_raw, w2_scales)
        nc.gpsimd.dma_start(w2_words_raw[:].bitcast(I32), words_of(w2_words))

        gain16 = new([P, PACK], F32, "gain16")
        nc.scalar.activation(gain16[:], gain[:], ACT.Copy, scale=0.0625)

        def gather(table, offsets, dtype, name):
            picked = new([P, S], dtype, name)
            nc.vector.tensor_copy(picked[:], table[:].indirect(offsets[:]))
            return picked

        d_bytes_picked = gather(d_byte_table, k1_list, U8, "d_bytes_picked")
        d_bytes = new([P, S], U8, "d_bytes")
        deal(d_bytes[:], d_bytes_picked[:])
        for j in range(2):
            nc.scalar.dma_start(d_bytes[:].bitcast(I32)[2 + j : P : 32, :], d_bytes[:].bitcast(I32)[16 + j : P : 32, :])
        d_words_picked = gather(d_word_table, k1_list, U32, "d_words_picked")
        d_codes = new([P, S], U32, "d_codes")
        deal(d_codes[:], d_words_picked[:])
        x2_bytes = gather(x_byte_table, two_list, U8, "x2_bytes")
        x2_codes = gather(x_word_table, two_list, U32, "x2_codes")

        def product(bank, codes, scale_bytes, t, moving_codes, moving_bytes):
            cols = slice(t * P, (t + 1) * P)
            nc.tensor.matmul_mx(
                out=bank, lhsT=codes[:, cols].bitcast(FP8X4), lhsT_scale=scale_bytes[:, cols],
                rhs=moving_codes.bitcast(FP8X4), rhs_scale=moving_bytes, start=True, stop=True,
            )

        d_window, tanh_neg = [], []
        for t in range(PACK):
            bank = psum.tile([P, S], F32, name=f"d_bank{t}", tag=f"bank{t}")
            product(bank[:], d_codes, d_bytes, t, x2_codes[:], x2_bytes[:])
            d_window.append(new([P, S + SPARE], F32, f"d_window{t}"))
            nc.gpsimd.memset(d_window[t][:, S:], 0.0)
            nc.scalar.activation(d_window[t][:, :S], bank[:], ACT.Copy, scale=gain16[:, t : t + 1])
            tanh_neg.append(new([P, S], F32, f"tanh_neg{t}"))
            nc.scalar.activation(tanh_neg[t][:], bank[:], ACT.Tanh, scale=-0.0625)

        w1_codes = new([P, S], U32, "w1_codes")
        w1_bytes = new([P, S], U8, "w1_bytes")
        x1_codes = gather(x_word_table, offs_list, U32, "x1_codes")
        x1_bytes = gather(x_byte_table, offs_list, U8, "x1_bytes")
        deal(w1_codes[:], w1_words_raw[:])
        deal(w1_bytes[:], w1_bytes_raw[:])

        y_bank = []
        for t in range(PACK):
            y_bank.append(psum.tile([P, S], F32, name=f"y_bank{t}", tag=f"bank{PACK + t}"))
            product(y_bank[t][:], w1_codes, w1_bytes, t, x1_codes[:], x1_bytes[:])

        cross = new([P, PACK, S], F32, "cross")
        y_window = [new([P, S], F32, f"y_window{t}") for t in range(PACK)]
        for t in range(PACK):
            if t == 2:
                for late in (2, 3):
                    nc.vector.tensor_scalar(y_window[late][:], y_bank[late][:], gain[:, late : late + 1], None, ALU.mult)
            nc.vector.tensor_tensor(cross[:, t, :], d_window[t][:].indirect(n2_list[:]), tanh_neg[t][:], ALU.mult)
        for t in range(2):
            nc.scalar.activation(y_window[t][:], y_bank[t][:], ACT.Copy, scale=gain[:, t : t + 1])

        w2_codes = new([P, S], U32, "w2_codes")
        z_codes = new([P, S], U32, "z_codes")
        z_bytes = new([P, S], U8, "z_bytes")
        w2_bytes = new([P, S], U8, "w2_bytes")
        deal(w2_bytes[:], w2_bytes_raw[:], nc.gpsimd)
        deal(w2_codes[:], w2_words_raw[:], nc.gpsimd)
        y_picked = []
        for u in range(HALVES):
            y_picked.append(new([P, PACK, half], F32, f"y_picked{u}"))
            for t in range(PACK):
                offsets = n1_list[:, u * half // 16 : (u + 1) * half // 16]
                nc.scalar.activation(y_picked[u][:, t, :], y_window[t][:].indirect(offsets), ACT.Copy)
        h_window = [new([P, S], F32, f"h_window{t}") for t in range(PACK)]
        h_bank = {}
        for u in range(HALVES):
            cols = slice(u * half, (u + 1) * half)
            z_rounded = new([P, half, PACK], BF16, f"z_rounded{u}", tag="z_rounded")
            nc.vector.tensor_tensor(
                z_rounded[:].rearrange("p (c i) t -> p c t i", i=4),
                y_picked[u][:].rearrange("p t (c i) -> p c t i", i=4),
                cross[:, :, cols].rearrange("p t (c i) -> p c t i", i=4),
                ALU.add,
            )
            nc.vector.quantize_mx(
                out=z_codes[:, cols].bitcast(FP8X4), scales=z_bytes[:, cols],
                in_=z_rounded[:].rearrange("p c t -> p (c t)"),
            )
            for t in range(PACK):
                h_bank[u, t] = psum.tile([P, half], F32, name=f"h_bank{u}_{t}", tag=f"bank{u * PACK + t}")
                product(h_bank[u, t][:], w2_codes, w2_bytes, t, z_codes[:, cols], z_bytes[:, cols])
                if u == 0:
                    nc.scalar.copy(h_window[t][:, cols], h_bank[u, t][:])

        out_rows = out_0.rearrange("(p t) c -> p t c", t=PACK)
        out_planes = new([P, PACK, S], BF16, "out_planes")
        placed = [new([P, S], F32, f"placed{t}") for t in range(PACK)]
        total = [new([P, PAIRS], F32, f"total{t}") for t in range(PACK)]

        pair = [new([P, 2, PAIRS], F32, f"pair{t}") for t in range(PACK)]

        def place_differences(t):
            nc.scalar.copy(h_window[t][:, half:], h_bank[1, t][:])
            nc.scalar.activation(pair[t][:, 0, :], h_window[t][:].indirect(n3_list[:]), ACT.Copy, scale=-0.5)
            if t == 0:
                nc.vector.tensor_copy(pair[t][:, 1, :], h_window[t][:].indirect(n4_list[:]))
            else:
                nc.scalar.activation(pair[t][:, 1, :], h_window[t][:].indirect(n4_list[:]), ACT.Copy)
            nc.vector.tensor_tensor(placed[t][:].indirect(n4_list[:]), pair[t][:, 1, :], pair[t][:, 0, :], ALU.add)

        def sum_squares(t):
            squares = new([P, 2, PAIRS], F32, f"squares{t}")
            if t == 0:
                nc.scalar.activation(squares[:], pair[t][:], ACT.Square)
                nc.vector.scalar_tensor_tensor(total[t][:], squares[:, 0, :], 4.0, squares[:, 1, :], ALU.mult, ALU.add)
            else:
                nc.scalar.activation(squares[:, 0, :], pair[t][:, 0, :], ACT.Square, scale=2.0)
                nc.scalar.activation(squares[:, 1, :], pair[t][:, 1, :], ACT.Square)
                nc.gpsimd.tensor_tensor(total[t][:], squares[:, 0, :], squares[:, 1, :], ALU.add)

        def place_roots(t):
            root = new([P, PAIRS], F32, f"root{t}")
            nc.scalar.activation(root[:], total[t][:], ACT.Sqrt, bias=0.25)
            nc.vector.tensor_copy(placed[t][:].indirect(n3_list[:]), root[:])
            nc.sync.dma_start(out_rows[:, t, :], placed[t][:])

        place_differences(0)
        place_differences(1)
        sum_squares(0)
        place_differences(2)
        place_roots(0)
        sum_squares(1)
        place_differences(3)
        sum_squares(2)
        place_roots(1)
        sum_squares(3)
        place_roots(2)
        place_roots(3)
        for t in range(PACK - 1):
            nc.scalar.copy(out_planes[:, t, :], placed[t][:])
        split = 336
        nc.vector.tensor_copy(out_planes[:, PACK - 1, :split], placed[PACK - 1][:, :split])
        nc.scalar.copy(out_planes[:, PACK - 1, split:], placed[PACK - 1][:, split:])

        out_rounded = new([P, S, PACK], BF16, "out_rounded")
        out_codes = new([P, S], U32, "out_codes")
        out_bytes = new([P, S], U8, "out_bytes")
        walk_out = out_rounded[:].rearrange("p (c i) t -> p c t i", i=4)
        walk_in = out_planes[:].rearrange("p t (c i) -> p c t i", i=4)
        nc.vector.tensor_copy(walk_out[:, : split // 4], walk_in[:, : split // 4])
        nc.scalar.copy(walk_out[:, split // 4 :], walk_in[:, split // 4 :])
        for cols in (slice(0, half), slice(half, S)):
            nc.vector.quantize_mx(
                out=out_codes[:, cols].bitcast(FP8X4), scales=out_bytes[:, cols],
                in_=out_rounded[:, cols, :].rearrange("p c t -> p (c t)"),
            )
            nc.sync.dma_start(words_of(out_1)[:, cols], out_codes[:].bitcast(I32)[:, cols])
        scale_rows = out_2[0].bitcast(I32)
        for q in range(4):
            queue = nc.scalar if q % 2 else nc.sync
            queue.dma_start(scale_rows[4 * q : 4 * q + 4, :], out_bytes[:].bitcast(I32)[32 * q : 32 * q + 4, :])
